import numpy as np, ml_dtypes
CORES = [125,109,93,77,61,45,29,13,114,98,82,66,50,34,18,2]
N = 16
W, H, TIMES = 1024, 1, 3
WTS = [1,1,1]
def setup_inputs(rng):
    return {"x": rng.standard_normal((N, 128, W), dtype=np.float32).astype(ml_dtypes.bfloat16)}
def reference(x):
    g = np.concatenate(list(x.astype(np.float64)), axis=1)
    for _ in range(TIMES):
        p = np.concatenate([g[:, -H:], g, g[:, :H]], axis=1)
        g = sum(WTS[i] * p[:, i:i + N * W] for i in range(2 * H + 1))
    return {"y": np.stack([g[:, W * r:W * r + W] for r in range(N)]).astype(ml_dtypes.bfloat16 if x.dtype != np.float64 else np.float64)}

@@ -1,0 +1,218 @@
+W = 1024
+HALO = 3
+TAPS = 2 * HALO + 1
+P = 128
+BLK_OUT = P - 2 * HALO
+NPAIR = 4
+EDGE = (W - 2 * NPAIR * BLK_OUT) // 2
+STRIP = EDGE + HALO
+EW = 2 * (STRIP + HALO)
+X0 = EDGE - HALO
+PAIR_OUT = 2 * BLK_OUT
+CB0 = P + TAPS - 1
+LQ = CB0 + P
+
+SCRATCH = {
+    "X": ("sbuf", [P, W], "bfloat16"),
+    "E": ("sbuf", [P, EW], "bfloat16"),
+    "A": ("sbuf", [P, LQ], "bfloat16"),
+    "CB": ("sbuf", [P, LQ], "bfloat16"),
+    "XT": ("sbuf", [P, W], "bfloat16"),
+    "ET": ("sbuf", [P, P], "bfloat16"),
+    "Y": ("sbuf", [P, W], "bfloat16"),
+    "YE": ("sbuf", [P, 64], "bfloat16"),
+    "D": ("dram", [P * LQ], "bfloat16"),
+    "DE": ("dram", [P, HALO], "bfloat16"),
+    "RL": ("dram", [P, HALO], "bfloat16"),
+}
+for _i in range(NPAIR):
+    SCRATCH["PA%d" % _i] = ("psum", [P, 512], "float32")
+    SCRATCH["PC%d" % _i] = ("psum", [P, 512], "float32")
+
+SEMAPHORES = ["ldD", "ldEL", "ldER", "ms", "go", "d1", "d2", "hL", "hR", "sent", "rin", "rout", "st",
+              "tE1", "cE1", "tE2", "cE2"]
+for _i in range(NPAIR):
+    SEMAPHORES += ["ldX%d" % _i, "t1_%d" % _i, "c1_%d" % _i, "t2_%d" % _i, "c2_%d" % _i]
+
+
+def _engines(mask):
+    return bin(mask).count("1")
+
+
+def _conv(a, b):
+    out = [0] * (len(a) + len(b) - 1)
+    for i, u in enumerate(a):
+        for j, v in enumerate(b):
+            out[i + j] += u * v
+    return out
+
+
+def _routes(T, topo):
+    cores = list(T.cores)
+    n = len(cores)
+    used = []
+    out = []
+    for r in range(n):
+        for step, side in ((1, "L"), (-1, "R")):
+            src, dst = cores[r], cores[(r + step) % n]
+            relay = None
+            if not topo.may_write(src, dst):
+                cand = [c for c in range(topo.CHIPS * topo.CORES_PER_CHIP)
+                        if c not in cores and c not in used and topo.may_write(src, c) and topo.may_write(c, dst)]
+                relay = min(cand, key=lambda c: (not topo.mates(topo.chip(c), topo.chip(dst)),
+                                                 topo.die(c) != topo.die(dst), c))
+                used.append(relay)
+            out.append((src, dst, side, relay))
+    return out
+
+
+def _write(g, topo, src, dst, out_ap, in_ap, remote_sem, local_sem):
+    rid, pid, _ = topo.addr(dst)
+    m = topo.mask(src, dst)
+    g.remote_dma(out_ap=out_ap, in_ap=in_ap, remote_sem=remote_sem, local_sem=local_sem, pid=pid, routing_id=rid,
+                 dma_engine_mask=m)
+    return _engines(m)
+
+
+def _halo_slot(T, side):
+    return T.E[:, 0:HALO] if side == "L" else T.E[:, EW - HALO:EW]
+
+
+def rank_program(g, core, T, topo):
+    S = T.sem
+    routes = _routes(T, topo)
+    rank = T.rank_of(core)
+
+    if rank is None:
+        for src, dst, side, relay in routes:
+            if relay == core:
+                g.wait_ge(S.rin, _engines(topo.mask(src, core)))
+                k = _write(g, topo, core, dst, _halo_slot(T, side), T.RL[:], S["h" + side], S.rout)
+                g.wait_ge(S.rout, k)
+        return
+
+    wts = [1]
+    for _ in range(HALO):
+        wts = _conv(wts, T.tables["WTS"])
+
+    mine = sorted([r for r in routes if r[0] == core], key=lambda r: r[3] is None)
+    sy, sc, te, ve = g.sync, g.scalar, g.tensor, g.vector
+
+    nm = 0
+    fills = [(slice(0, 1), 1.0), (slice(1, P), 0.0), (slice(CB0 + 1, LQ), 0.0)]
+    for d in range(HALO + 1):
+        a, b = CB0 - (TAPS - 1 - d), CB0 - d
+        if a == b:
+            fills.append((slice(a, a + 1), float(wts[d])))
+        elif wts[d] == wts[TAPS - 1 - d]:
+            fills.append((slice(a, b + 1, b - a), float(wts[d])))
+        else:
+            fills.append((slice(b, b + 1), float(wts[d])))
+            fills.append((slice(a, a + 1), float(wts[TAPS - 1 - d])))
+    for sl, v in fills:
+        ve.memset(T.A[:, sl], v).then_inc(S.ms, 1)
+        nm += 1
+
+    for src, dst, side, relay in mine:
+        if relay is not None:
+            cols = T.x[:, W - HALO:W] if side == "L" else T.x[:, 0:HALO]
+            sy.dma_start(T.DE[:], cols).then_inc(S.ldD, 16)
+    sy.dma_start(T.E[:, HALO:HALO + STRIP], T.x[:, 0:STRIP]).then_inc(S.ldEL, 16)
+    sc.dma_start(T.E[:, HALO + STRIP:EW - HALO], T.x[:, W - STRIP:W]).then_inc(S.ldER, 16)
+
+    sc.wait_ge(S.ms, nm)
+    sc.dma_start(T.D[:], T.A[:]).then_inc(S.d1, 16)
+    sc.sem_inc(S.go, 1)
+    sc.wait_ge(S.d1, 16)
+    sc.dma_start(T.CB[:, 0:LQ - 1], T.D[0:P * (LQ - 1)]).then_inc(S.d2, 16)
+
+    bounds = [X0] + [X0 + PAIR_OUT * (p + 1) + 2 * HALO for p in range(NPAIR)]
+    sy.wait_ge(S.go, 1)
+    for p in range(NPAIR):
+        sy.dma_start(T.X[:, bounds[p]:bounds[p + 1]], T.x[:, bounds[p]:bounds[p + 1]]).then_inc(S["ldX%d" % p], 16)
+
+    sent = 0
+    for src, dst, side, relay in mine:
+        if relay is not None:
+            g.wait_ge(S.ldD, 16)
+            sent += _write(g, topo, core, relay, T.RL[:], T.DE[:], S.rin, S.sent)
+        elif side == "L":
+            g.wait_ge(S.ldER, 16)
+            sent += _write(g, topo, core, dst, _halo_slot(T, side), T.E[:, EW - 2 * HALO:EW - HALO], S.hL, S.sent)
+        else:
+            g.wait_ge(S.ldEL, 16)
+            sent += _write(g, topo, core, dst, _halo_slot(T, side), T.E[:, HALO:2 * HALO], S.hR, S.sent)
+
+    ident = T.CB[:, 0:P]
+    band = T.CB[:, CB0:CB0 + BLK_OUT]
+
+    def t1(p):
+        te.wait_ge(S["ldX%d" % p], 16)
+        for j in range(2):
+            c0 = X0 + BLK_OUT * (2 * p + j)
+            te.matmul(T["PA%d" % p][:, P * j:P * (j + 1)], T.X[:, c0:c0 + P], ident, True, True).then_inc(
+                S["t1_%d" % p], 1)
+
+    def t2(p):
+        te.wait_ge(S["c1_%d" % p], 1)
+        for j in range(2):
+            b = 2 * p + j
+            te.matmul(T["PC%d" % p][:, BLK_OUT * j:BLK_OUT * (j + 1)], T.XT[:, P * b:P * (b + 1)], band, True,
+                      True).then_inc(S["t2_%d" % p], 1)
+
+    te.wait_ge(S.d2, 16)
+    t1(0)
+    t1(1)
+    t2(0)
+    t1(2)
+    t2(1)
+    t1(3)
+    t2(2)
+    t2(3)
+    arrive = {}
+    for src, dst, side, relay in routes:
+        if dst == core:
+            arrive[side] = _engines(topo.mask(src if relay is None else relay, core))
+    te.wait_ge(S.ldEL, 16)
+    te.wait_ge(S.ldER, 16)
+    te.wait_ge(S.hL, arrive["L"])
+    te.wait_ge(S.hR, arrive["R"])
+    te.matmul(T.PA0[0:EW, 0:P], T.E[:], ident, True, True).then_inc(S.tE1, 1)
+    te.wait_ge(S.cE1, 1)
+    te.wait_ge(S.c2_0, 1)
+    ne = EW - 2 * HALO
+    te.matmul(T.PC0[:, 0:ne], T.ET[0:EW, :], T.CB[0:EW, CB0:CB0 + ne], True, True).then_inc(S.tE2, 1)
+
+    def c1(p):
+        ve.wait_ge(S["t1_%d" % p], 2)
+        ve.tensor_copy(T.XT[:, 2 * P * p:2 * P * (p + 1)], T["PA%d" % p][:, 0:2 * P]).then_inc(S["c1_%d" % p], 1)
+
+    def c2(p):
+        ve.wait_ge(S["t2_%d" % p], 2)
+        ve.tensor_copy(T.Y[:, 256 * p:256 * p + PAIR_OUT], T["PC%d" % p][:, 0:PAIR_OUT]).then_inc(S["c2_%d" % p], 1)
+
+    c1(0)
+    c1(1)
+    c2(0)
+    c1(2)
+    c2(1)
+    c1(3)
+    c2(2)
+    c2(3)
+    ve.wait_ge(S.tE1, 1)
+    ve.tensor_copy(T.ET[0:EW, :], T.PA0[0:EW, 0:P]).then_inc(S.cE1, 1)
+    ve.wait_ge(S.tE2, 1)
+    ve.tensor_copy(T.YE[:, 0:ne], T.PC0[:, 0:ne]).then_inc(S.cE2, 1)
+
+    for p in range(NPAIR):
+        q = sy if p % 2 == 0 else sc
+        q.wait_ge(S["c2_%d" % p], 1)
+        q.dma_start(T.y[:, EDGE + PAIR_OUT * p:EDGE + PAIR_OUT * (p + 1)],
+                    T.Y[:, 256 * p:256 * p + PAIR_OUT]).then_inc(S.st, 16)
+    sy.wait_ge(S.cE2, 1)
+    sy.dma_start(T.y[:, 0:EDGE], T.YE[:, 0:EDGE]).then_inc(S.st, 16)
+    sc.wait_ge(S.cE2, 1)
+    sc.dma_start(T.y[:, W - EDGE:W], T.YE[:, ne - EDGE:ne]).then_inc(S.st, 16)
+
+    g.wait_ge(S.sent, sent)
+    g.wait_ge(S.st, 16 * (NPAIR + 2))

@@ -1,3 +1,5 @@
+from concourse.mybir import AluOpType
+
 W = 1024
 HALO = 3
 TAPS = 2 * HALO + 1
@@ -9,28 +11,34 @@ STRIP = EDGE + HALO
 EW = 2 * (STRIP + HALO)
 X0 = EDGE - HALO
 PAIR_OUT = 2 * BLK_OUT
-CB0 = P + TAPS - 1
-LQ = CB0 + P
+LQ = P + 1
+NBIT = 7
 
 SCRATCH = {
     "X": ("sbuf", [P, W], "bfloat16"),
     "E": ("sbuf", [P, EW], "bfloat16"),
     "A": ("sbuf", [P, LQ], "bfloat16"),
-    "CB": ("sbuf", [P, LQ], "bfloat16"),
+    "B": ("sbuf", [P, P], "bfloat16"),
     "XT": ("sbuf", [P, W], "bfloat16"),
     "ET": ("sbuf", [P, P], "bfloat16"),
     "Y": ("sbuf", [P, W], "bfloat16"),
     "YE": ("sbuf", [P, 64], "bfloat16"),
+    "NEG": ("sbuf", [P, P], "bfloat16"),
+    "ONE": ("sbuf", [P, P], "bfloat16"),
+    "ZERO": ("sbuf", [P, P], "bfloat16"),
+    "ID": ("sbuf", [P, P], "bfloat16"),
     "D": ("dram", [P * LQ], "bfloat16"),
     "DE": ("dram", [P, HALO], "bfloat16"),
     "RL": ("dram", [P, HALO], "bfloat16"),
 }
+for _i in range(NBIT):
+    SCRATCH["S%d" % _i] = ("sbuf", [P, P >> (_i + 1), 2, 1 << _i], "bfloat16")
 for _i in range(NPAIR):
     SCRATCH["PA%d" % _i] = ("psum", [P, 512], "float32")
     SCRATCH["PC%d" % _i] = ("psum", [P, 512], "float32")
 
 SEMAPHORES = ["ldD", "ldEL", "ldER", "ms", "go", "d1", "d2", "hL", "hR", "sent", "rin", "rout", "st",
-              "tE1", "cE1", "tE2", "cE2"]
+              "tE1", "cE1", "tE2", "cE2", "mk", "tG", "cI"] + ["sb%d" % _b for _b in range(NBIT)]
 for _i in range(NPAIR):
     SEMAPHORES += ["ldX%d" % _i, "t1_%d" % _i, "c1_%d" % _i, "t2_%d" % _i, "c2_%d" % _i]
 
@@ -98,20 +106,28 @@ def rank_program(g, core, T, topo):
     mine = sorted([r for r in routes if r[0] == core], key=lambda r: r[3] is None)
     sy, sc, te, ve = g.sync, g.scalar, g.tensor, g.vector
 
-    nm = 0
-    fills = [(slice(0, 1), 1.0), (slice(1, P), 0.0), (slice(CB0 + 1, LQ), 0.0)]
+    pos = [(LQ - d) % LQ for d in range(TAPS)]
+    fills = [(slice(1, LQ - TAPS + 1), 0.0)]
     for d in range(HALO + 1):
-        a, b = CB0 - (TAPS - 1 - d), CB0 - d
+        a, b = sorted((pos[d], pos[TAPS - 1 - d]))
         if a == b:
             fills.append((slice(a, a + 1), float(wts[d])))
         elif wts[d] == wts[TAPS - 1 - d]:
             fills.append((slice(a, b + 1, b - a), float(wts[d])))
         else:
-            fills.append((slice(b, b + 1), float(wts[d])))
-            fills.append((slice(a, a + 1), float(wts[TAPS - 1 - d])))
+            fills.append((slice(pos[d], pos[d] + 1), float(wts[d])))
+            fills.append((slice(pos[TAPS - 1 - d], pos[TAPS - 1 - d] + 1), float(wts[TAPS - 1 - d])))
     for sl, v in fills:
         ve.memset(T.A[:, sl], v).then_inc(S.ms, 1)
-        nm += 1
+    for b in range(NBIT):
+        ve.memset(T["S%d" % b][0:1, :, 0, :], -1.0).then_inc(S["sb%d" % b], 1)
+        ve.memset(T["S%d" % b][0:1, :, 1, :], 1.0).then_inc(S["sb%d" % b], 1)
+    ve.memset(T.NEG[0:1, :], float(1 - NBIT)).then_inc(S.mk, 1)
+    ve.memset(T.ONE[0:1, :], 1.0).then_inc(S.mk, 1)
+    ve.memset(T.ZERO[:], 0.0).then_inc(S.mk, 1)
+    ve.wait_ge(S.mk, 3)
+    ve.wait_ge(S.tG, 1)
+    ve.tensor_tensor(T.ID[:], T.PC3[:, 0:P], T.ZERO[:], AluOpType.max).then_inc(S.cI, 1)
 
     for src, dst, side, relay in mine:
         if relay is not None:
@@ -120,11 +136,11 @@ def rank_program(g, core, T, topo):
     sy.dma_start(T.E[:, HALO:HALO + STRIP], T.x[:, 0:STRIP]).then_inc(S.ldEL, 16)
     sc.dma_start(T.E[:, HALO + STRIP:EW - HALO], T.x[:, W - STRIP:W]).then_inc(S.ldER, 16)
 
-    sc.wait_ge(S.ms, nm)
+    sc.wait_ge(S.ms, len(fills))
     sc.dma_start(T.D[:], T.A[:]).then_inc(S.d1, 16)
     sc.sem_inc(S.go, 1)
     sc.wait_ge(S.d1, 16)
-    sc.dma_start(T.CB[:, 0:LQ - 1], T.D[0:P * (LQ - 1)]).then_inc(S.d2, 16)
+    sc.dma_start(T.B[:], T.D[0:P * P]).then_inc(S.d2, 16)
 
     bounds = [X0] + [X0 + PAIR_OUT * (p + 1) + 2 * HALO for p in range(NPAIR)]
     sy.wait_ge(S.go, 1)
@@ -143,8 +159,8 @@ def rank_program(g, core, T, topo):
             g.wait_ge(S.ldEL, 16)
             sent += _write(g, topo, core, dst, _halo_slot(T, side), T.E[:, HALO:2 * HALO], S.hR, S.sent)
 
-    ident = T.CB[:, 0:P]
-    band = T.CB[:, CB0:CB0 + BLK_OUT]
+    ident = T.ID[:]
+    band = T.B[:, 0:BLK_OUT]
 
     def t1(p):
         te.wait_ge(S["ldX%d" % p], 16)
@@ -160,13 +176,20 @@ def rank_program(g, core, T, topo):
             te.matmul(T["PC%d" % p][:, BLK_OUT * j:BLK_OUT * (j + 1)], T.XT[:, P * b:P * (b + 1)], band, True,
                       True).then_inc(S["t2_%d" % p], 1)
 
-    te.wait_ge(S.d2, 16)
+    for b in range(NBIT):
+        te.wait_ge(S["sb%d" % b], 2)
+        row = T["S%d" % b][0:1, :, :, :]
+        te.matmul(T.PC3[:, 0:P], row, row, b == 0, False)
+    te.wait_ge(S.mk, 3)
+    te.matmul(T.PC3[:, 0:P], T.NEG[0:1, :], T.ONE[0:1, :], False, True).then_inc(S.tG, 1)
+    te.wait_ge(S.cI, 1)
     t1(0)
     t1(1)
-    t2(0)
     t1(2)
-    t2(1)
     t1(3)
+    te.wait_ge(S.d2, 16)
+    t2(0)
+    t2(1)
     t2(2)
     t2(3)
     arrive = {}
@@ -181,7 +204,7 @@ def rank_program(g, core, T, topo):
     te.wait_ge(S.cE1, 1)
     te.wait_ge(S.c2_0, 1)
     ne = EW - 2 * HALO
-    te.matmul(T.PC0[:, 0:ne], T.ET[0:EW, :], T.CB[0:EW, CB0:CB0 + ne], True, True).then_inc(S.tE2, 1)
+    te.matmul(T.PC0[:, 0:ne], T.ET[0:EW, :], T.B[0:EW, 0:ne], True, True).then_inc(S.tE2, 1)
 
     def c1(p):
         ve.wait_ge(S["t1_%d" % p], 2)
@@ -193,10 +216,10 @@ def rank_program(g, core, T, topo):
 
     c1(0)
     c1(1)
-    c2(0)
     c1(2)
-    c2(1)
     c1(3)
+    c2(0)
+    c2(1)
     c2(2)
     c2(3)
     ve.wait_ge(S.tE1, 1)

from concourse.mybir import AluOpType

W = 1024
HALO = 3
TAPS = 2 * HALO + 1
P = 128
BLK_OUT = P - 2 * HALO
NPAIR = 4
EDGE = (W - 2 * NPAIR * BLK_OUT) // 2
STRIP = EDGE + HALO
EW = 2 * (STRIP + HALO)
X0 = EDGE - HALO
PAIR_OUT = 2 * BLK_OUT
LQ = P + 1
NBIT = 7

SCRATCH = {
    "X": ("sbuf", [P, W], "bfloat16"),
    "E": ("sbuf", [P, EW], "bfloat16"),
    "A": ("sbuf", [P, LQ], "bfloat16"),
    "B": ("sbuf", [P, P], "bfloat16"),
    "XT": ("sbuf", [P, W], "bfloat16"),
    "ET": ("sbuf", [P, P], "bfloat16"),
    "Y": ("sbuf", [P, W], "bfloat16"),
    "YE": ("sbuf", [P, 64], "bfloat16"),
    "NEG": ("sbuf", [P, P], "bfloat16"),
    "ONE": ("sbuf", [P, P], "bfloat16"),
    "ZERO": ("sbuf", [P, P], "bfloat16"),
    "ID": ("sbuf", [P, P], "bfloat16"),
    "D": ("dram", [P * LQ], "bfloat16"),
    "DE": ("dram", [P, HALO], "bfloat16"),
    "RL": ("dram", [P, HALO], "bfloat16"),
}
for _i in range(NBIT):
    SCRATCH["S%d" % _i] = ("sbuf", [P, P >> (_i + 1), 2, 1 << _i], "bfloat16")
for _i in range(NPAIR):
    SCRATCH["PA%d" % _i] = ("psum", [P, 512], "float32")
    SCRATCH["PC%d" % _i] = ("psum", [P, 512], "float32")

SEMAPHORES = ["ldD", "ldEL", "ldER", "ms", "go", "d1", "d2", "hL", "hR", "sent", "rin", "rout", "st",
              "tE1", "cE1", "tE2", "cE2", "mk", "tG", "cI"] + ["sb%d" % _b for _b in range(NBIT)]
for _i in range(NPAIR):
    SEMAPHORES += ["ldX%d" % _i, "t1_%d" % _i, "c1_%d" % _i, "t2_%d" % _i, "c2_%d" % _i]


def _engines(mask):
    return bin(mask).count("1")


def _conv(a, b):
    out = [0] * (len(a) + len(b) - 1)
    for i, u in enumerate(a):
        for j, v in enumerate(b):
            out[i + j] += u * v
    return out


def _routes(T, topo):
    cores = list(T.cores)
    n = len(cores)
    used = []
    out = []
    for r in range(n):
        for step, side in ((1, "L"), (-1, "R")):
            src, dst = cores[r], cores[(r + step) % n]
            relay = None
            if not topo.may_write(src, dst):
                cand = [c for c in range(topo.CHIPS * topo.CORES_PER_CHIP)
                        if c not in cores and c not in used and topo.may_write(src, c) and topo.may_write(c, dst)]
                relay = min(cand, key=lambda c: (not topo.mates(topo.chip(c), topo.chip(dst)),
                                                 topo.die(c) != topo.die(dst), c))
                used.append(relay)
            out.append((src, dst, side, relay))
    return out


def _write(g, topo, src, dst, out_ap, in_ap, remote_sem, local_sem):
    rid, pid, _ = topo.addr(dst)
    m = topo.mask(src, dst)
    g.remote_dma(out_ap=out_ap, in_ap=in_ap, remote_sem=remote_sem, local_sem=local_sem, pid=pid, routing_id=rid,
                 dma_engine_mask=m)
    return _engines(m)


def _halo_slot(T, side):
    return T.E[:, 0:HALO] if side == "L" else T.E[:, EW - HALO:EW]


def rank_program(g, core, T, topo):
    S = T.sem
    routes = _routes(T, topo)
    rank = T.rank_of(core)

    if rank is None:
        for src, dst, side, relay in routes:
            if relay == core:
                g.wait_ge(S.rin, _engines(topo.mask(src, core)))
                k = _write(g, topo, core, dst, _halo_slot(T, side), T.RL[:], S["h" + side], S.rout)
                g.wait_ge(S.rout, k)
        return

    wts = [1]
    for _ in range(HALO):
        wts = _conv(wts, T.tables["WTS"])

    mine = sorted([r for r in routes if r[0] == core], key=lambda r: r[3] is None)
    sy, sc, te, ve = g.sync, g.scalar, g.tensor, g.vector

    pos = [(LQ - d) % LQ for d in range(TAPS)]
    fills = [(slice(1, LQ - TAPS + 1), 0.0)]
    for d in range(HALO + 1):
        a, b = sorted((pos[d], pos[TAPS - 1 - d]))
        if a == b:
            fills.append((slice(a, a + 1), float(wts[d])))
        elif wts[d] == wts[TAPS - 1 - d]:
            fills.append((slice(a, b + 1, b - a), float(wts[d])))
        else:
            fills.append((slice(pos[d], pos[d] + 1), float(wts[d])))
            fills.append((slice(pos[TAPS - 1 - d], pos[TAPS - 1 - d] + 1), float(wts[TAPS - 1 - d])))
    for sl, v in fills:
        ve.memset(T.A[:, sl], v).then_inc(S.ms, 1)
    for b in range(NBIT):
        ve.memset(T["S%d" % b][0:1, :, 0, :], -1.0).then_inc(S["sb%d" % b], 1)
        ve.memset(T["S%d" % b][0:1, :, 1, :], 1.0).then_inc(S["sb%d" % b], 1)
    ve.memset(T.NEG[0:1, :], float(1 - NBIT)).then_inc(S.mk, 1)
    ve.memset(T.ONE[0:1, :], 1.0).then_inc(S.mk, 1)
    ve.memset(T.ZERO[:], 0.0).then_inc(S.mk, 1)
    ve.wait_ge(S.mk, 3)
    ve.wait_ge(S.tG, 1)
    ve.tensor_tensor(T.ID[:], T.PC3[:, 0:P], T.ZERO[:], AluOpType.max).then_inc(S.cI, 1)

    for src, dst, side, relay in mine:
        if relay is not None:
            cols = T.x[:, W - HALO:W] if side == "L" else T.x[:, 0:HALO]
            sy.dma_start(T.DE[:], cols).then_inc(S.ldD, 16)
    sy.dma_start(T.E[:, HALO:HALO + STRIP], T.x[:, 0:STRIP]).then_inc(S.ldEL, 16)
    sc.dma_start(T.E[:, HALO + STRIP:EW - HALO], T.x[:, W - STRIP:W]).then_inc(S.ldER, 16)

    sc.wait_ge(S.ms, len(fills))
    sc.dma_start(T.D[:], T.A[:]).then_inc(S.d1, 16)
    sc.sem_inc(S.go, 1)
    sc.wait_ge(S.d1, 16)
    sc.dma_start(T.B[:], T.D[0:P * P]).then_inc(S.d2, 16)

    bounds = [X0] + [X0 + PAIR_OUT * (p + 1) + 2 * HALO for p in range(NPAIR)]
    sy.wait_ge(S.go, 1)
    for p in range(NPAIR):
        sy.dma_start(T.X[:, bounds[p]:bounds[p + 1]], T.x[:, bounds[p]:bounds[p + 1]]).then_inc(S["ldX%d" % p], 16)

    sent = 0
    for src, dst, side, relay in mine:
        if relay is not None:
            g.wait_ge(S.ldD, 16)
            sent += _write(g, topo, core, relay, T.RL[:], T.DE[:], S.rin, S.sent)
        elif side == "L":
            g.wait_ge(S.ldER, 16)
            sent += _write(g, topo, core, dst, _halo_slot(T, side), T.E[:, EW - 2 * HALO:EW - HALO], S.hL, S.sent)
        else:
            g.wait_ge(S.ldEL, 16)
            sent += _write(g, topo, core, dst, _halo_slot(T, side), T.E[:, HALO:2 * HALO], S.hR, S.sent)

    ident = T.ID[:]
    band = T.B[:, 0:BLK_OUT]

    def t1(p):
        te.wait_ge(S["ldX%d" % p], 16)
        for j in range(2):
            c0 = X0 + BLK_OUT * (2 * p + j)
            te.matmul(T["PA%d" % p][:, P * j:P * (j + 1)], T.X[:, c0:c0 + P], ident, True, True).then_inc(
                S["t1_%d" % p], 1)

    def t2(p):
        te.wait_ge(S["c1_%d" % p], 1)
        for j in range(2):
            b = 2 * p + j
            te.matmul(T["PC%d" % p][:, BLK_OUT * j:BLK_OUT * (j + 1)], T.XT[:, P * b:P * (b + 1)], band, True,
                      True).then_inc(S["t2_%d" % p], 1)

    for b in range(NBIT):
        te.wait_ge(S["sb%d" % b], 2)
        row = T["S%d" % b][0:1, :, :, :]
        te.matmul(T.PC3[:, 0:P], row, row, b == 0, False)
    te.wait_ge(S.mk, 3)
    te.matmul(T.PC3[:, 0:P], T.NEG[0:1, :], T.ONE[0:1, :], False, True).then_inc(S.tG, 1)
    te.wait_ge(S.cI, 1)
    t1(0)
    t1(1)
    t1(2)
    t1(3)
    te.wait_ge(S.d2, 16)
    t2(0)
    t2(1)
    t2(2)
    t2(3)
    arrive = {}
    for src, dst, side, relay in routes:
        if dst == core:
            arrive[side] = _engines(topo.mask(src if relay is None else relay, core))
    te.wait_ge(S.ldEL, 16)
    te.wait_ge(S.ldER, 16)
    te.wait_ge(S.hL, arrive["L"])
    te.wait_ge(S.hR, arrive["R"])
    te.matmul(T.PA0[0:EW, 0:P], T.E[:], ident, True, True).then_inc(S.tE1, 1)
    te.wait_ge(S.cE1, 1)
    te.wait_ge(S.c2_0, 1)
    ne = EW - 2 * HALO
    te.matmul(T.PC0[:, 0:ne], T.ET[0:EW, :], T.B[0:EW, 0:ne], True, True).then_inc(S.tE2, 1)

    def c1(p):
        ve.wait_ge(S["t1_%d" % p], 2)
        ve.tensor_copy(T.XT[:, 2 * P * p:2 * P * (p + 1)], T["PA%d" % p][:, 0:2 * P]).then_inc(S["c1_%d" % p], 1)

    def c2(p):
        ve.wait_ge(S["t2_%d" % p], 2)
        ve.tensor_copy(T.Y[:, 256 * p:256 * p + PAIR_OUT], T["PC%d" % p][:, 0:PAIR_OUT]).then_inc(S["c2_%d" % p], 1)

    c1(0)
    c1(1)
    c1(2)
    c1(3)
    c2(0)
    c2(1)
    c2(2)
    c2(3)
    ve.wait_ge(S.tE1, 1)
    ve.tensor_copy(T.ET[0:EW, :], T.PA0[0:EW, 0:P]).then_inc(S.cE1, 1)
    ve.wait_ge(S.tE2, 1)
    ve.tensor_copy(T.YE[:, 0:ne], T.PC0[:, 0:ne]).then_inc(S.cE2, 1)

    for p in range(NPAIR):
        q = sy if p % 2 == 0 else sc
        q.wait_ge(S["c2_%d" % p], 1)
        q.dma_start(T.y[:, EDGE + PAIR_OUT * p:EDGE + PAIR_OUT * (p + 1)],
                    T.Y[:, 256 * p:256 * p + PAIR_OUT]).then_inc(S.st, 16)
    sy.wait_ge(S.cE2, 1)
    sy.dma_start(T.y[:, 0:EDGE], T.YE[:, 0:EDGE]).then_inc(S.st, 16)
    sc.wait_ge(S.cE2, 1)
    sc.dma_start(T.y[:, W - EDGE:W], T.YE[:, ne - EDGE:ne]).then_inc(S.st, 16)

    g.wait_ge(S.sent, sent)
    g.wait_ge(S.st, 16 * (NPAIR + 2))
